import numpy as np, ml_dtypes
CORES = [16,23,24,31,64,71]
N = 6
import mx_ref
NC, KT, G, ROOT = 512, 1, 4, 4
C = np.float32(0.043)
BF = ml_dtypes.bfloat16
def cut(t, i, w=512):
    return t[:, w * i:w * i + w]
def tile(rs):
    return np.stack(rs, axis=2).reshape(128, -1).astype(BF)
def layer(w, X):
    out = []
    for i in range(G):
        for t in range(len(X)):
            p = mx_ref.matmul(mx_ref.quantize(cut(w, len(X) * i + t)), X[t])
            z = p if t == 0 else z + p
        out.append(z)
    return out
def act(Z):
    return [np.maximum(z, 0) * C for z in Z]
def setup_inputs(rng):
    def f(*shape):
        return mx_ref.flush((rng.standard_normal(shape, dtype=np.float32) * np.exp2(rng.integers(-2, 3, shape[:-1] + (1,)))).astype(BF))
    return {"x": f(N, 128, KT * 4 * NC), "w1": f(N, 128, G * KT * 512), "w2": f(N, 128, 512)}
def setup_inputs_blocks(rng):
    d = setup_inputs(rng)
    for k in ("x", "w1", "w2"): d[k] = mx_ref.spread(d[k], rng, 4)
    return d
def setup_inputs_wide(rng):
    d = setup_inputs(rng)
    for k in ("x", "w1", "w2"): d[k] = mx_ref.flush((d[k].astype(np.float32) * np.exp2(rng.integers(-8, 9, (N, 1, 1))).astype(np.float32)).astype(BF))
    return d
def setup_inputs_zeros(rng):
    d = setup_inputs(rng); v = d["x"].reshape(N, 128, -1, 4).copy()
    v[np.broadcast_to((rng.random((N, 1, v.shape[2], 1)) < 0.33), v.shape)] = 0
    d["x"] = v.reshape(d["x"].shape)
    return d
def reference(x, w1, w2):
    h = mx_ref.quantize(tile(act(layer(w1[ROOT], [mx_ref.quantize(cut(x[ROOT], t, 4 * NC)) for t in range(KT)]))))
    y = np.zeros((N, 128, NC), np.float32)
    for r in range(N):
        y[r] = mx_ref.matmul(mx_ref.quantize(w2[r]), h)
    return {"y": y}

from concourse.bass import DstId, RemoteDMATransfer
from concourse.mybir import dt, AluOpType, ActivationFunctionType

NC = 512
G = 4
C = 0.043
CC = ((0, 128), (128, 384), (384, 512))
PIECES = (("c", 0, 128), ("c", 128, 384), ("p", 0, 512), ("c", 384, 512))
YP = ((0, 384), (384, 512))

SCRATCH = {
    "xs": ("sbuf", [128, 4 * NC], "bfloat16"),
    "w1s": ("sbuf", [128, G * 512], "bfloat16"),
    "w2s": ("sbuf", [128, 512], "bfloat16"),
    "xq": ("sbuf", [128, NC], "float8_e4m3fn_x4"),
    "xp": ("sbuf", [128, NC], "uint8"),
    "w1q": ("sbuf", [128, G * 128], "float8_e4m3fn_x4"),
    "w1p": ("sbuf", [128, G * 128], "uint8"),
    "w2q": ("sbuf", [128, 128], "float8_e4m3fn_x4"),
    "w2p": ("sbuf", [128, 128], "uint8"),
    "ht": ("sbuf", [128, 4 * NC], "bfloat16"),
    "hq": ("sbuf", [128, NC], "float8_e4m3fn_x4"),
    "hp": ("sbuf", [128, NC], "uint8"),
    "ys": ("sbuf", [128, NC], "float32"),
    "ps": ("psum", [128, 8 * 512], "float32"),
}
SEMAPHORES = (
    ["ldw1", "ldw2", "qv", "sent"]
    + ["ldx%d" % c for c in range(len(CC))]
    + ["qx%d" % c for c in range(len(CC))]
    + ["qw%d" % b for b in range(G)]
    + ["mm%d_%d" % (c, b) for c in range(len(CC)) for b in range(G)]
    + ["act%d" % c for c in range(len(CC))]
    + ["qh%d" % c for c in range(len(CC))]
    + ["in%d" % k for k in range(len(PIECES))]
    + ["ym%d" % j for j in range(len(YP))]
    + ["yc%d" % j for j in range(len(YP))]
    + ["st%d" % j for j in range(len(YP))]
)


def ones(m):
    return bin(m).count("1")


def tree(T, topo):
    cores = list(T.cores)
    root = cores[T.root]
    rest = [c for c in cores if c != root]
    near = [c for c in rest if topo.may_write(root, c)]
    far = [c for c in rest if not topo.may_write(root, c)]
    kids = {c: [] for c in cores}
    gates = []
    for ch in sorted({topo.chip(c) for c in near}):
        here = [c for c in near if topo.chip(c) == ch]
        able = [c for c in here if all(topo.may_write(c, f) for f in far)]
        gate = (able or here)[0]
        gates.append(gate)
        kids[root].append(gate)
        kids[gate] += [c for c in here if c != gate]
    for f in far:
        able = [x for x in gates if topo.may_write(x, f)]
        pick = min(able, key=lambda x: (len([k for k in kids[x] if topo.chip(k) != topo.chip(x)]),
                                        0 if topo.mates(topo.chip(x), topo.chip(f)) else 1))
        kids[pick].append(f)
    up = {k: p for p in cores for k in kids[p]}
    return root, up, kids


def lanes(topo, src, dsts):
    out, used = {}, 0
    for k in sorted(dsts, key=lambda k: ones(topo.mask(src, k))):
        out[k] = topo.mask(src, k) & ~used
        used |= out[k]
    return out


def rank_program(g, core, T, topo):
    if T.rank_of(core) is None:
        return
    S = T.sem
    root, up, kids = tree(T, topo)
    mine = lanes(topo, core, kids[core])
    total = len(PIECES) * sum(ones(m) for m in mine.values())
    v, s, t, q = g.vector, g.scalar, g.tensor, g.sync

    def view(k):
        kind, a, e = PIECES[k]
        return T.hq[:, a:e].bitcast(dt.uint8) if kind == "c" else T.hp[:, a:e]

    def push(k):
        trs = []
        for d in kids[core]:
            rid, pid, _ring = topo.addr(d)
            trs.append(RemoteDMATransfer(dst_ids=[DstId(rid=rid, pnc=pid)], dma_engine_mask=mine[d],
                                         remote_sem=S["in%d" % k], src=view(k), dst=view(k)))
        g.remote_dma_fused(trs, local_sem=S.sent)

    if core == root:
        for c, (a, e) in enumerate(CC):
            q.dma_start(T.xs[:, 4 * a:4 * e], T.x[:, 4 * a:4 * e]).then_inc(S["ldx%d" % c], 16)
            if c == 0:
                s.dma_start(T.w1s[:], T.w1[:]).then_inc(S.ldw1, 16)
        q.dma_start(T.w2s[:], T.w2[:]).then_inc(S.ldw2, 16)

        def quant_x(c):
            a, e = CC[c]
            v.wait_ge(S["ldx%d" % c], 16)
            v.quantize_mx(T.xq[:, a:e], T.xp[:, a:e], T.xs[:, 4 * a:4 * e]).then_inc(S["qx%d" % c], 1)

        quant_x(0)
        v.wait_ge(S.ldw1, 16)
        for b in range(G):
            v.quantize_mx(T.w1q[:, 128 * b:128 * b + 128], T.w1p[:, 128 * b:128 * b + 128],
                          T.w1s[:, 512 * b:512 * b + 512]).then_inc(S["qw%d" % b], 1)

        for c, (a, e) in enumerate(CC):
            n = e - a
            t.wait_ge(S["qx%d" % c], 1)
            if c >= 2:
                t.wait_ge(S["act%d" % (c - 2)], G)
            for b in range(G):
                if c == 0:
                    t.wait_ge(S["qw%d" % b], 1)
                z = 512 * (G * (c % 2) + b)
                t.matmul_mx(T.ps[:, z:z + n], T.w1q[:, 128 * b:128 * b + 128], T.w1p[:, 128 * b:128 * b + 128],
                            T.xq[:, a:e], T.xp[:, a:e], True, True).then_inc(S["mm%d_%d" % (c, b)], 1)
            for b in range(G - 1):
                z = 512 * (G * (c % 2) + b)
                s.wait_ge(S["mm%d_%d" % (c, b)], 1)
                s.activation(T.ht[:, 4 * a + b:4 * e:4], T.ps[:, z:z + n], ActivationFunctionType.Relu,
                             scale=C).then_inc(S["act%d" % c], 1)
            if c >= 1 and c + 1 < len(CC):
                quant_x(c + 1)
            b = G - 1
            z = 512 * (G * (c % 2) + b)
            v.wait_ge(S["mm%d_%d" % (c, b)], 1)
            v.tensor_scalar(T.ht[:, 4 * a + b:4 * e:4], T.ps[:, z:z + n], 0.0, C,
                            AluOpType.max, AluOpType.mult).then_inc(S["act%d" % c], 1)
            v.wait_ge(S["act%d" % c], G)
            v.quantize_mx(T.hq[:, a:e], T.hp[:, a:e], T.ht[:, 4 * a:4 * e]).then_inc(S["qh%d" % c], 1)
            if c == 0 and len(CC) > 1:
                quant_x(1)
        seen = 0
        for k, (_kind, a, e) in enumerate(PIECES):
            need = max(c for c, (ca, ce) in enumerate(CC) if ca < e and a < ce) + 1
            for c in range(seen, need):
                g.wait_ge(S["qh%d" % c], 1)
            seen = max(seen, need)
            push(k)
    else:
        q.dma_start(T.w2s[:], T.w2[:]).then_inc(S.ldw2, 16)
        n_in = ones(lanes(topo, up[core], kids[up[core]])[core])
        if kids[core]:
            for k in range(len(PIECES)):
                g.wait_ge(S["in%d" % k], n_in)
                push(k)

    v.wait_ge(S.ldw2, 16)
    v.quantize_mx(T.w2q[:], T.w2p[:], T.w2s[:]).then_inc(S.qv, 1)
    t.wait_ge(S.qv, 1)
    have = set()
    for j, (a, e) in enumerate(YP):
        if core == root:
            want = [("qh%d" % c, 1) for c in range(len(CC))]
        else:
            want = [("in%d" % k, n_in) for k, (_kind, pa, pe) in enumerate(PIECES) if pa < e and a < pe]
        for name, n in want:
            if name not in have:
                t.wait_ge(S[name], n)
                have.add(name)
        t.matmul_mx(T.ps[:, 512 * j:512 * j + e - a], T.w2q[:], T.w2p[:], T.hq[:, a:e], T.hp[:, a:e],
                    True, True).then_inc(S["ym%d" % j], 1)
    for j, (a, e) in enumerate(YP):
        if j % 2 == 0:
            v.wait_ge(S["ym%d" % j], 1)
            v.tensor_copy(T.ys[:, a:e], T.ps[:, 512 * j:512 * j + e - a]).then_inc(S["yc%d" % j], 1)
            d = q
        else:
            s.wait_ge(S["ym%d" % j], 1)
            s.activation(T.ys[:, a:e], T.ps[:, 512 * j:512 * j + e - a],
                         ActivationFunctionType.Copy).then_inc(S["yc%d" % j], 1)
            d = s
        if not total:
            d.wait_ge(S["yc%d" % j], 1)
            d.dma_start(T.y[:, a:e], T.ys[:, a:e]).then_inc(S["st%d" % j], 16)
    if total:
        for j in range(len(YP)):
            q.wait_ge(S["yc%d" % j], 1)
        q.wait_ge(S.sent, total)
        q.dma_start(T.y[:], T.ys[:]).then_inc(S.st0, 16)
        q.wait_ge(S.st0, 16)
        g.wait_ge(S.sent, total)
    else:
        for j in range(len(YP)):
            (q if j % 2 == 0 else s).wait_ge(S["st%d" % j], 16)
